import numpy as np
import ml_dtypes


def mxq(x, axis, fmt="e4m3"):
    dtype, down = {"e4m3": (ml_dtypes.float8_e4m3fn, 7), "e5m2": (ml_dtypes.float8_e5m2, 14)}[fmt]
    v = np.moveaxis(np.asarray(x, np.float32).astype(ml_dtypes.bfloat16).astype(np.float64), axis, -1)
    blocks = v.reshape(v.shape[:-1] + (-1, 32))
    amax = np.abs(blocks).max(-1, keepdims=True)
    byte = np.maximum(np.where(amax > 0, np.frexp(amax)[1] - 1 + 127, 0) - down, 1)
    scale = np.exp2(byte - 127.0)
    codes = (blocks / scale).astype(np.float32).astype(dtype).astype(np.float64)
    return np.moveaxis((codes * scale).reshape(v.shape), -1, axis)


WIDE = False


def mx_kscale(k):
    if not WIDE:
        return np.ones(k)
    levels = np.array([10, -10, 5, -5, 0])
    if k % 512:
        return np.exp2(np.random.permutation(np.resize(levels, k // 32))).repeat(32)
    a = np.empty((k // 512, 16))
    for p in range(k // 512):
        a[p, :8] = np.random.permutation(np.resize(levels, 8))
        for g in range(8):
            far = levels[np.abs(levels - a[p, g]) >= 10]
            a[p, g + 8] = far[np.random.randint(len(far))]
    return np.exp2(a.ravel()).repeat(32)


def f64(x):
    return np.asarray(x).astype(np.float64)


def striped(idx):
    return np.tile(idx.reshape(-1, 16).T, (8, 1)).astype(np.uint16)


def unstriped(offs):
    return offs[:16].T.reshape(-1).astype(np.int64)


def relu(v):
    return np.maximum(v, 0.0)


def d_relu(v):
    return (v > 0).astype(np.float64)


K, T, E, C, H, N = 384, 512, 6, 256, 512, 512
TOP = 3


def by_expert(wq, xq):
    return np.concatenate([wq[e].T @ xq[:, e * C:(e + 1) * C] for e in range(E)], axis=1)


def setup_inputs():
    n = np.random.standard_normal
    s = mx_kscale(N)[:, None]
    u = mx_kscale(H)
    deal = np.repeat(np.arange(E), C).reshape(TOP, T)[:, np.random.permutation(T)]
    deal = np.take_along_axis(deal, np.argsort(np.random.rand(TOP, T), axis=0), axis=0)
    for _ in range(8):
        s_, t_ = np.random.permutation(T).reshape(2, -1); r = np.random.randint(TOP, size=T // 2); x, y = deal[r, s_].copy(), deal[r, t_].copy()
        ok = ~((deal[:, s_] == y).any(0) | (deal[:, t_] == x).any(0)); deal[r[ok], s_[ok]] = y[ok]; deal[r[ok], t_[ok]] = x[ok]
    order = np.lexsort((np.random.rand(TOP * T), deal.reshape(-1)))
    slot_token = order % T; pos = np.empty(TOP * T, np.int64); pos[order] = np.arange(TOP * T); pos = pos.reshape(TOP, T)
    g = np.random.uniform(0.5, 1.5, (TOP, T)); g = g / g.sum(0)
    w_slot = np.empty(E * C)
    for r in range(TOP): w_slot[pos[r]] = g[r]
    return {
        "dyT": (n((N, T)) * s).astype(np.float32),
        "a1": n((H, E * C)).astype(np.float32),
        "a3": n((H, E * C)).astype(np.float32),
        "w2": (n((E, N, H)) / np.sqrt(N) / s[None] * u[None, None, :]).astype(np.float32),
        "w1": (n((E, H, K)) / np.sqrt(H) / u[None, :, None]).astype(np.float32),
        "w3": (n((E, H, K)) / np.sqrt(H) / u[None, :, None]).astype(np.float32),
        "gate": np.tile(w_slot, (N, 1)).astype(np.float32),
        "offs": striped(slot_token),
        "pos1": striped(pos[0]),
        "pos2": striped(pos[1]),
        "pos3": striped(pos[2]),
    }


def reference(dyT, a1, a3, w2, w1, w3, gate, offs, pos1, pos2, pos3):
    idx = unstriped(offs)
    gq = mxq(f64(gate) * f64(dyT)[:, idx], 0, "e4m3")
    dh = by_expert(mxq(f64(w2), 1, "e4m3"), gq)
    da1 = dh * f64(a3) * d_relu(f64(a1))
    da3 = dh * relu(f64(a1))
    dx = by_expert(mxq(f64(w1), 1, "e4m3"), mxq(da1, 0, "e4m3")) + by_expert(mxq(f64(w3), 1, "e4m3"), mxq(da3, 0, "e4m3"))
    return dx[:, unstriped(pos1)] + dx[:, unstriped(pos2)] + dx[:, unstriped(pos3)]

@@ -1,0 +1,200 @@
+from contextlib import ExitStack
+
+import concourse.mybir as mybir
+
+K, T, E, C, H, N = 384, 512, 6, 256, 512, 512
+S = E * C
+FLOPS = 2 * S * (N * H + 2 * H * K)
+BYTES = 4 * (N * T + 2 * H * S + E * N * H + 2 * E * H * K + 128 * S + K * T) + 2 * 128 * (S + 3 * T) // 16
+
+F32 = mybir.dt.float32
+BF16 = mybir.dt.bfloat16
+U32 = mybir.dt.uint32
+U16 = mybir.dt.uint16
+U8 = mybir.dt.uint8
+FP8X4 = mybir.dt.float8_e4m3fn_x4
+ALU = mybir.AluOpType
+
+P = 128
+PACK = 4
+KT = K // P
+LIST_COLS = C // 16
+WHOLE = 4
+
+
+def tile_moe_bdx_glu_relu_kernel(
+    tc, dyT, a1, a3, w2, w1, w3, gate, offs, pos1, pos2, pos3, out
+):
+    nc = tc.nc
+    with ExitStack() as ctx:
+        keep = ctx.enter_context(tc.tile_pool(name="keep", bufs=1))
+        ring = ctx.enter_context(tc.tile_pool(name="ring", bufs=2))
+        psum = ctx.enter_context(tc.psum_pool(name="psum", bufs=4))
+
+        offs_sb = keep.tile([P, S // 16], U16, name="offs_sb")
+        pos_sb = [keep.tile([P, T // 16], U16, name="pos_sb%d" % r) for r in range(3)]
+        dy_sb = [keep.tile([P, T], F32, name="dy_sb%d" % j) for j in range(PACK)]
+        gate_head = keep.tile([P, 2 * C], F32, name="gate_head")
+        gate_rest = keep.tile([P, S - 2 * C], F32, name="gate_rest")
+        dx_sb = [keep.tile([P, S], F32, name="dx_sb%d" % kt) for kt in range(KT)]
+
+        w2_raw, a_raw, w13_raw = {}, {}, {}
+        da_q = {}
+
+        def load_w2(e):
+            raw = ring.tile([P, PACK, H], F32, name="w2_raw", bufs=3)
+            nc.sync.dma_start(out=raw[:], in_=w2[e].rearrange("(p j) i -> p j i", j=PACK))
+            w2_raw[e] = raw
+
+        def load_a(e):
+            pair = []
+            for src in (a1, a3):
+                raw = ring.tile([P, PACK, C], F32, name="a_raw", bufs=10)
+                rows = src.rearrange("(p t) s -> p t s", t=PACK)
+                nc.sync.dma_start(out=raw[:], in_=rows[:, :, e * C : (e + 1) * C])
+                pair.append(raw)
+            a_raw[e] = pair
+
+        def load_w13(e, k0, width):
+            pair = []
+            for src in (w1, w3):
+                raw = ring.tile([P, PACK, width], F32, name="w13_raw%d" % width, bufs=4 if width == K else 6)
+                rows = src[e].rearrange("(p t) k -> p t k", t=PACK)
+                nc.sync.dma_start(out=raw[:], in_=rows[:, :, k0 : k0 + width])
+                pair.append(raw)
+            w13_raw[(e, k0)] = pair
+
+        def quantize(grouped, words, name, bufs, cuts):
+            codes = ring.tile([P, words], U32, name=name + "_codes", bufs=bufs, align_bytes=64)
+            scales = ring.tile([P, words], U8, name=name + "_scales", bufs=bufs, align_bytes=64)
+            for lo, hi in cuts:
+                nc.vector.quantize_mx(
+                    out=codes[:, lo:hi].bitcast(FP8X4),
+                    scales=scales[:, lo:hi],
+                    in_=grouped[:, PACK * lo : PACK * hi],
+                )
+            return codes, scales
+
+        def rows_by_four(ap):
+            return ap.rearrange("p t (c i) -> p c t i", i=4)
+
+        def words_by_four(ap):
+            return ap.rearrange("p (c i t) -> p c t i", i=4, t=PACK)
+
+        def first_layer(e):
+            if e < 2:
+                gate_e = gate_head[:, e * C : (e + 1) * C]
+            else:
+                gate_e = gate_rest[:, (e - 2) * C : (e - 1) * C]
+            g32 = ring.tile([P, PACK, C], F32, name="g32", bufs=3)
+            for j in range(PACK):
+                window = dy_sb[j][:].indirect(offs_sb[:, e * LIST_COLS : (e + 1) * LIST_COLS])
+                nc.vector.tensor_tensor(g32[:, j, :], window, gate_e, ALU.mult)
+            g16 = ring.tile([P, PACK * C], BF16, name="g16", bufs=2, align_bytes=64)
+            nc.scalar.copy(out=words_by_four(g16[:]), in_=rows_by_four(g32[:]))
+            g_codes, g_scales = quantize(g16, C, "g", E, [(0, C)])
+
+            w2_16 = ring.tile([P, PACK * H], BF16, name="w2_16", bufs=2, align_bytes=64)
+            nc.scalar.copy(
+                out=w2_16[:].rearrange("p (t m j) -> p m j t", t=PACK, j=PACK),
+                in_=w2_raw[e][:].rearrange("p j (m t) -> p m j t", t=PACK),
+            )
+            w_codes, w_scales = quantize(w2_16, H, "w2", 3, [(0, H)])
+
+            a1_e, a3_e = a_raw[e]
+            live = ring.tile([P, PACK, C], F32, name="live", bufs=2)
+            for half in range(2):
+                dh = psum.tile([P, 2, C], F32, name="dh")
+                for u in range(2):
+                    cols = slice((2 * half + u) * P, (2 * half + u + 1) * P)
+                    nc.tensor.matmul_mx(
+                        out=dh[:, u, :],
+                        lhsT=w_codes[:, cols].bitcast(FP8X4),
+                        lhsT_scale=w_scales[:, cols],
+                        rhs=g_codes[:].bitcast(FP8X4),
+                        rhs_scale=g_scales[:],
+                        start=True,
+                        stop=True,
+                    )
+                planes = slice(2 * half, 2 * half + 2)
+                nc.vector.scalar_tensor_tensor(
+                    out=live[:, planes, :], in0=a1_e[:, planes, :], scalar=0.0, in1=dh[:], op0=ALU.is_gt, op1=ALU.mult
+                )
+            da16 = ring.tile([P, 2 * PACK * C], BF16, name="da16", bufs=2, align_bytes=64)
+            for w, factor in enumerate((a3_e, a1_e)):
+                nc.vector.tensor_tensor(
+                    words_by_four(da16[:, w * PACK * C : (w + 1) * PACK * C]),
+                    rows_by_four(live[:]),
+                    rows_by_four(factor[:]),
+                    ALU.mult,
+                )
+            da_q[e] = quantize(da16, 2 * C, "da", 4, [(0, 2 * C)])
+
+        def second_layer(e, k0, width):
+            w16 = ring.tile([P, 2 * PACK * width], BF16, name="w13_16_%d" % width, bufs=2 if width == K else 3, align_bytes=64)
+            for w in range(2):
+                nc.scalar.copy(
+                    out=words_by_four(w16[:, w * PACK * width : (w + 1) * PACK * width]),
+                    in_=rows_by_four(w13_raw[(e, k0)][w][:]),
+                )
+            cuts = [(0, 512), (512, 768)] if width == K else [(0, 2 * width)]
+            w_codes, w_scales = quantize(w16, 2 * width, "w13_%d" % width, 2 if width == K else 3, cuts)
+            da_codes, da_scales = da_q[e]
+            for k in range(0, width, P):
+                dx = psum.tile([P, C], F32, name="dx")
+                for w in range(2):
+                    cols = slice(w * width + k, w * width + k + P)
+                    slots = slice(w * C, (w + 1) * C)
+                    nc.tensor.matmul_mx(
+                        out=dx[:],
+                        lhsT=w_codes[:, cols].bitcast(FP8X4),
+                        lhsT_scale=w_scales[:, cols],
+                        rhs=da_codes[:, slots].bitcast(FP8X4),
+                        rhs_scale=da_scales[:, slots],
+                        start=(w == 0),
+                        stop=(w == 1),
+                    )
+                nc.scalar.copy(out=dx_sb[(k0 + k) // P][:, e * C : (e + 1) * C], in_=dx[:])
+
+        def combine(kt):
+            picked = [ring.tile([P, T], F32, name="a_raw", bufs=10) for r in range(3)]
+            for r in range(3):
+                nc.vector.tensor_copy(picked[r][:], dx_sb[kt][:].indirect(pos_sb[r][:]))
+                if r == 2:
+                    nc.vector.tensor_tensor(picked[0][:], picked[0][:], picked[1][:], ALU.add)
+            nc.vector.tensor_tensor(picked[0][:], picked[0][:], picked[2][:], ALU.add)
+            nc.sync.dma_start(out=out[kt * P : (kt + 1) * P, :], in_=picked[0][:])
+
+        dy_rows = dyT.rearrange("(p j) t -> p j t", j=PACK)
+        nc.sync.dma_start(offs_sb[:], offs)
+        nc.sync.dma_start(out=gate_head[:], in_=gate[0:P, 0 : 2 * C])
+        for j in range(PACK):
+            nc.sync.dma_start(out=dy_sb[j][:], in_=dy_rows[:, j, :])
+        load_w2(0)
+        nc.sync.dma_start(out=gate_rest[:], in_=gate[0:P, 2 * C : S])
+        load_a(0)
+        load_w2(1)
+        load_a(1)
+        for r, pos in enumerate((pos1, pos2, pos3)):
+            nc.sync.dma_start(pos_sb[r][:], pos)
+        first_layer(0)
+        load_w2(2)
+        first_layer(1)
+        for e in range(2, E):
+            if e < E - 1:
+                load_w13(e - 2, 0, K)
+            load_a(e)
+            if e < E - 1:
+                load_w2(e + 1)
+            first_layer(e)
+            if e < E - 1:
+                second_layer(e - 2, 0, K)
+        load_w13(WHOLE - 1, 0, K)
+        second_layer(WHOLE - 1, 0, K)
+        for kt in range(KT):
+            for e in range(WHOLE, E):
+                load_w13(e, kt * P, P)
+        for kt in range(KT):
+            for e in range(WHOLE, E):
+                second_layer(e, kt * P, P)
+            combine(kt)

@@ -1,6 +1,7 @@
 from contextlib import ExitStack
 
 import concourse.mybir as mybir
+from concourse.masks import make_identity
 
 K, T, E, C, H, N = 384, 512, 6, 256, 512, 512
 S = E * C
@@ -19,7 +20,7 @@ P = 128
 PACK = 4
 KT = K // P
 LIST_COLS = C // 16
-WHOLE = 4
+AHEAD = 3
 
 
 def tile_moe_bdx_glu_relu_kernel(
@@ -29,51 +30,60 @@ def tile_moe_bdx_glu_relu_kernel(
     with ExitStack() as ctx:
         keep = ctx.enter_context(tc.tile_pool(name="keep", bufs=1))
         ring = ctx.enter_context(tc.tile_pool(name="ring", bufs=2))
-        psum = ctx.enter_context(tc.psum_pool(name="psum", bufs=4))
+        psum = ctx.enter_context(tc.psum_pool(name="psum", bufs=3))
 
         offs_sb = keep.tile([P, S // 16], U16, name="offs_sb")
         pos_sb = [keep.tile([P, T // 16], U16, name="pos_sb%d" % r) for r in range(3)]
         dy_sb = [keep.tile([P, T], F32, name="dy_sb%d" % j) for j in range(PACK)]
-        gate_head = keep.tile([P, 2 * C], F32, name="gate_head")
-        gate_rest = keep.tile([P, S - 2 * C], F32, name="gate_rest")
+        gate_sb = [keep.tile([P, C], F32, name="gate_sb%d" % e) for e in range(E)]
         dx_sb = [keep.tile([P, S], F32, name="dx_sb%d" % kt) for kt in range(KT)]
+        ident = keep.tile([P, P], F32, name="ident")
+        make_identity(nc, ident[:])
 
         w2_raw, a_raw, w13_raw = {}, {}, {}
-        da_q = {}
+        g32, g16, g_q, w2_16, w2_q, dh, live, da16, da_q, w13_16, w13_q, dx = ({} for i in range(12))
+        picked, turned, total = {}, {}, {}
 
         def load_w2(e):
-            raw = ring.tile([P, PACK, H], F32, name="w2_raw", bufs=3)
-            nc.sync.dma_start(out=raw[:], in_=w2[e].rearrange("(p j) i -> p j i", j=PACK))
-            w2_raw[e] = raw
+            w2_raw[e] = ring.tile([P, PACK, H], F32, name="w2_raw", bufs=3)
+            nc.sync.dma_start(out=w2_raw[e][:], in_=w2[e].rearrange("(p j) i -> p j i", j=PACK))
+
+        def load_gate(e):
+            if e < E:
+                nc.sync.dma_start(out=gate_sb[e][:], in_=gate[0:P, e * C : (e + 1) * C])
 
         def load_a(e):
-            pair = []
-            for src in (a1, a3):
-                raw = ring.tile([P, PACK, C], F32, name="a_raw", bufs=10)
+            for w, src in enumerate((a1, a3)):
+                a_raw[e, w] = ring.tile([P, PACK, C], F32, name="a_raw", bufs=10)
                 rows = src.rearrange("(p t) s -> p t s", t=PACK)
-                nc.sync.dma_start(out=raw[:], in_=rows[:, :, e * C : (e + 1) * C])
-                pair.append(raw)
-            a_raw[e] = pair
+                nc.sync.dma_start(out=a_raw[e, w][:], in_=rows[:, :, e * C : (e + 1) * C])
 
         def load_w13(e, k0, width):
-            pair = []
-            for src in (w1, w3):
-                raw = ring.tile([P, PACK, width], F32, name="w13_raw%d" % width, bufs=4 if width == K else 6)
+            for w, src in enumerate((w1, w3)):
+                w13_raw[e, k0, w] = ring.tile([P, PACK, width], F32, name="w13_raw%d" % width, bufs=4 if width == K else 6)
                 rows = src[e].rearrange("(p t) k -> p t k", t=PACK)
-                nc.sync.dma_start(out=raw[:], in_=rows[:, :, k0 : k0 + width])
-                pair.append(raw)
-            w13_raw[(e, k0)] = pair
+                nc.sync.dma_start(out=w13_raw[e, k0, w][:], in_=rows[:, :, k0 : k0 + width])
 
-        def quantize(grouped, words, name, bufs, cuts):
+        def mx_tiles(words, name, bufs):
             codes = ring.tile([P, words], U32, name=name + "_codes", bufs=bufs, align_bytes=64)
             scales = ring.tile([P, words], U8, name=name + "_scales", bufs=bufs, align_bytes=64)
-            for lo, hi in cuts:
-                nc.vector.quantize_mx(
-                    out=codes[:, lo:hi].bitcast(FP8X4),
-                    scales=scales[:, lo:hi],
-                    in_=grouped[:, PACK * lo : PACK * hi],
-                )
             return codes, scales
+
+        def quantize(pair, grouped, lo, hi):
+            nc.vector.quantize_mx(
+                out=pair[0][:, lo:hi].bitcast(FP8X4), scales=pair[1][:, lo:hi], in_=grouped[:, PACK * lo : PACK * hi]
+            )
+
+        def product(dst, left, cols, right, slots, start, stop):
+            nc.tensor.matmul_mx(
+                out=dst,
+                lhsT=left[0][:, cols].bitcast(FP8X4),
+                lhsT_scale=left[1][:, cols],
+                rhs=right[0][:, slots].bitcast(FP8X4),
+                rhs_scale=right[1][:, slots],
+                start=start,
+                stop=stop,
+            )
 
         def rows_by_four(ap):
             return ap.rearrange("p t (c i) -> p c t i", i=4)
@@ -81,120 +91,195 @@ def tile_moe_bdx_glu_relu_kernel(
         def words_by_four(ap):
             return ap.rearrange("p (c i t) -> p c t i", i=4, t=PACK)
 
-        def first_layer(e):
-            if e < 2:
-                gate_e = gate_head[:, e * C : (e + 1) * C]
-            else:
-                gate_e = gate_rest[:, (e - 2) * C : (e - 1) * C]
-            g32 = ring.tile([P, PACK, C], F32, name="g32", bufs=3)
-            for j in range(PACK):
-                window = dy_sb[j][:].indirect(offs_sb[:, e * LIST_COLS : (e + 1) * LIST_COLS])
-                nc.vector.tensor_tensor(g32[:, j, :], window, gate_e, ALU.mult)
-            g16 = ring.tile([P, PACK * C], BF16, name="g16", bufs=2, align_bytes=64)
-            nc.scalar.copy(out=words_by_four(g16[:]), in_=rows_by_four(g32[:]))
-            g_codes, g_scales = quantize(g16, C, "g", E, [(0, C)])
+        def gather_g(e, j):
+            if e >= E:
+                return
+            if j == 0:
+                g32[e] = ring.tile([P, PACK, C], F32, name="g32", bufs=2)
+            window = dy_sb[j][:].indirect(offs_sb[:, e * LIST_COLS : (e + 1) * LIST_COLS])
+            nc.vector.tensor_tensor(g32[e][:, j, :], window, gate_sb[e][:], ALU.mult)
 
-            w2_16 = ring.tile([P, PACK * H], BF16, name="w2_16", bufs=2, align_bytes=64)
+        def round_g(e):
+            if e >= E:
+                return
+            g16[e] = ring.tile([P, PACK * C], BF16, name="g16", bufs=2, align_bytes=64)
+            nc.scalar.copy(out=words_by_four(g16[e][:]), in_=rows_by_four(g32[e][:]))
+
+        def quantize_g(e):
+            if e >= E:
+                return
+            g_q[e] = mx_tiles(C, "g", 2)
+            quantize(g_q[e], g16[e], 0, C)
+
+        def round_w2(e):
+            if e >= E:
+                return
+            w2_16[e] = ring.tile([P, PACK * H], BF16, name="w2_16", bufs=2, align_bytes=64)
             nc.scalar.copy(
-                out=w2_16[:].rearrange("p (t m j) -> p m j t", t=PACK, j=PACK),
+                out=w2_16[e][:].rearrange("p (t m j) -> p m j t", t=PACK, j=PACK),
                 in_=w2_raw[e][:].rearrange("p j (m t) -> p m j t", t=PACK),
             )
-            w_codes, w_scales = quantize(w2_16, H, "w2", 3, [(0, H)])
 
-            a1_e, a3_e = a_raw[e]
-            live = ring.tile([P, PACK, C], F32, name="live", bufs=2)
+        def quantize_w2(e):
+            if e >= E:
+                return
+            w2_q[e] = mx_tiles(H, "w2", 2)
+            quantize(w2_q[e], w2_16[e], 0, H)
+
+        def multiply_w2(e):
+            if e >= E:
+                return
             for half in range(2):
-                dh = psum.tile([P, 2, C], F32, name="dh")
-                for u in range(2):
-                    cols = slice((2 * half + u) * P, (2 * half + u + 1) * P)
-                    nc.tensor.matmul_mx(
-                        out=dh[:, u, :],
-                        lhsT=w_codes[:, cols].bitcast(FP8X4),
-                        lhsT_scale=w_scales[:, cols],
-                        rhs=g_codes[:].bitcast(FP8X4),
-                        rhs_scale=g_scales[:],
-                        start=True,
-                        stop=True,
-                    )
-                planes = slice(2 * half, 2 * half + 2)
-                nc.vector.scalar_tensor_tensor(
-                    out=live[:, planes, :], in0=a1_e[:, planes, :], scalar=0.0, in1=dh[:], op0=ALU.is_gt, op1=ALU.mult
-                )
-            da16 = ring.tile([P, 2 * PACK * C], BF16, name="da16", bufs=2, align_bytes=64)
-            for w, factor in enumerate((a3_e, a1_e)):
-                nc.vector.tensor_tensor(
-                    words_by_four(da16[:, w * PACK * C : (w + 1) * PACK * C]),
-                    rows_by_four(live[:]),
-                    rows_by_four(factor[:]),
-                    ALU.mult,
-                )
-            da_q[e] = quantize(da16, 2 * C, "da", 4, [(0, 2 * C)])
+                dh[e, half] = psum.tile([P, PACK, P], F32, name="dh", bufs=2)
+                for t in range(PACK):
+                    product(dh[e, half][:, t, :], w2_q[e], slice(t * P, (t + 1) * P), g_q[e], slice(half * P, (half + 1) * P), True, True)
 
-        def second_layer(e, k0, width):
-            w16 = ring.tile([P, 2 * PACK * width], BF16, name="w13_16_%d" % width, bufs=2 if width == K else 3, align_bytes=64)
+        def mask_dh(e):
+            for half in range(2):
+                live[e, half] = ring.tile([P, PACK, P], F32, name="live", bufs=2)
+                nc.vector.scalar_tensor_tensor(
+                    out=live[e, half][:],
+                    in0=a_raw[e, 0][:, :, half * P : (half + 1) * P],
+                    scalar=0.0,
+                    in1=dh[e, half][:],
+                    op0=ALU.is_gt,
+                    op1=ALU.mult,
+                )
+
+        def make_da(e):
+            da16[e] = ring.tile([P, 2 * PACK * C], BF16, name="da16", bufs=1, align_bytes=64)
+            for w in (1, 0):
+                for half in range(2):
+                    lo = PACK * (w * C + half * P)
+                    nc.vector.tensor_tensor(
+                        words_by_four(da16[e][:, lo : lo + PACK * P]),
+                        rows_by_four(live[e, half][:]),
+                        rows_by_four(a_raw[e, 1 - w][:, :, half * P : (half + 1) * P]),
+                        ALU.mult,
+                    )
+
+        def quantize_da(e):
+            da_q[e] = mx_tiles(2 * C, "da", 3)
+            for w in (1, 0):
+                quantize(da_q[e], da16[e], w * C, (w + 1) * C)
+
+        def round_w13(e, k0, width):
+            if e < 0:
+                return
+            w13_16[e, k0] = ring.tile([P, 2 * PACK * width], BF16, name="w13_16_%d" % width, bufs=2 if width == K else 3, align_bytes=64)
             for w in range(2):
                 nc.scalar.copy(
-                    out=words_by_four(w16[:, w * PACK * width : (w + 1) * PACK * width]),
-                    in_=rows_by_four(w13_raw[(e, k0)][w][:]),
+                    out=words_by_four(w13_16[e, k0][:, w * PACK * width : (w + 1) * PACK * width]),
+                    in_=rows_by_four(w13_raw[e, k0, w][:]),
                 )
-            cuts = [(0, 512), (512, 768)] if width == K else [(0, 2 * width)]
-            w_codes, w_scales = quantize(w16, 2 * width, "w13_%d" % width, 2 if width == K else 3, cuts)
-            da_codes, da_scales = da_q[e]
+
+        def quantize_w13(e, k0, width, part):
+            if e < 0:
+                return
+            if part == 0:
+                w13_q[e, k0] = mx_tiles(2 * width, "w13_%d" % width, 2 if width == K else 3)
+            lo, hi = ((0, 512), (512, 768))[part] if width == K else (0, 2 * width)
+            quantize(w13_q[e, k0], w13_16[e, k0], lo, hi)
+
+        def multiply_w13(e, k0, width):
+            if e < 0:
+                return
             for k in range(0, width, P):
-                dx = psum.tile([P, C], F32, name="dx")
+                dx[e, k0 + k] = psum.tile([P, C], F32, name="dx", bufs=4)
                 for w in range(2):
                     cols = slice(w * width + k, w * width + k + P)
-                    slots = slice(w * C, (w + 1) * C)
-                    nc.tensor.matmul_mx(
-                        out=dx[:],
-                        lhsT=w_codes[:, cols].bitcast(FP8X4),
-                        lhsT_scale=w_scales[:, cols],
-                        rhs=da_codes[:, slots].bitcast(FP8X4),
-                        rhs_scale=da_scales[:, slots],
-                        start=(w == 0),
-                        stop=(w == 1),
-                    )
-                nc.scalar.copy(out=dx_sb[(k0 + k) // P][:, e * C : (e + 1) * C], in_=dx[:])
+                    product(dx[e, k0 + k][:], w13_q[e, k0], cols, da_q[e], slice(w * C, (w + 1) * C), w == 0, w == 1)
 
-        def combine(kt):
-            picked = [ring.tile([P, T], F32, name="a_raw", bufs=10) for r in range(3)]
-            for r in range(3):
-                nc.vector.tensor_copy(picked[r][:], dx_sb[kt][:].indirect(pos_sb[r][:]))
-                if r == 2:
-                    nc.vector.tensor_tensor(picked[0][:], picked[0][:], picked[1][:], ALU.add)
-            nc.vector.tensor_tensor(picked[0][:], picked[0][:], picked[2][:], ALU.add)
-            nc.sync.dma_start(out=out[kt * P : (kt + 1) * P, :], in_=picked[0][:])
+        def empty_dx(e, k0, width):
+            if e < 0:
+                return
+            for k in range(k0, k0 + width, P):
+                nc.scalar.copy(out=dx_sb[k // P][:, e * C : (e + 1) * C], in_=dx[e, k][:])
+
+        def pick(kt, r, lo, hi):
+            picked[kt, r, lo] = ring.tile([P, hi - lo], F32, name="a_raw", bufs=10)
+            nc.vector.tensor_copy(picked[kt, r, lo][:], dx_sb[kt][:].indirect(pos_sb[r][:, lo // 16 : hi // 16]))
+
+        def add(kt, r, lo):
+            nc.vector.tensor_tensor(picked[kt, 0, lo][:], picked[kt, 0, lo][:], picked[kt, r, lo][:], ALU.add)
+
+        def store(kt, lo, hi, src):
+            nc.sync.dma_start(out=out[kt * P : (kt + 1) * P, lo:hi], in_=src[:])
+
+        def add_on_tensor(kt, lo, hi):
+            blocks = (hi - lo) // P
+            summed = psum.tile([P, blocks, P], F32, name="dh", bufs=2)
+            for b in range(blocks):
+                for r in range(3):
+                    nc.tensor.matmul(
+                        summed[:, b, :], picked[kt, r, lo][:, b * P : (b + 1) * P], ident[:],
+                        start=(r == 0), stop=(r == 2), is_transpose=True,
+                    )
+            turned = ring.tile([P, blocks, P], F32, name="turned", bufs=2)
+            nc.scalar.copy(out=turned[:], in_=summed[:])
+            back = psum.tile([P, blocks, P], F32, name="dh", bufs=2)
+            for b in range(blocks):
+                nc.tensor.transpose(back[:, b, :], turned[:, b, :], ident[:])
+            result = ring.tile([P, blocks, P], F32, name="result", bufs=2)
+            nc.scalar.copy(out=result[:], in_=back[:])
+            nc.scalar.dma_start(out=out[kt * P : (kt + 1) * P, lo:hi].rearrange("p (b t) -> p b t", t=P), in_=result[:])
 
         dy_rows = dyT.rearrange("(p j) t -> p j t", j=PACK)
         nc.sync.dma_start(offs_sb[:], offs)
-        nc.sync.dma_start(out=gate_head[:], in_=gate[0:P, 0 : 2 * C])
-        for j in range(PACK):
+        load_gate(0)
+        nc.sync.dma_start(out=dy_sb[0][:], in_=dy_rows[:, 0, :])
+        load_gate(1)
+        for j in range(1, PACK):
+            if j == PACK - 1:
+                load_w2(0)
             nc.sync.dma_start(out=dy_sb[j][:], in_=dy_rows[:, j, :])
-        load_w2(0)
-        nc.sync.dma_start(out=gate_rest[:], in_=gate[0:P, 2 * C : S])
-        load_a(0)
-        load_w2(1)
-        load_a(1)
+        for j in range(PACK):
+            for e in range(2):
+                gather_g(e, j)
+        round_w2(0)
+        round_g(0)
+        quantize_w2(0)
+        quantize_g(0)
+        multiply_w2(0)
+        round_g(1)
+        last = E - 1
+        for e in range(E):
+            if e > 0:
+                load_w13(e - 1, 0, K)
+            load_gate(e + 2)
+            if e < last:
+                load_w2(e + 1)
+            load_a(e)
+            round_w13(e - 1, 0, K)
+            for j in range(PACK):
+                gather_g(e + 2, j)
+            quantize_w13(e - 1, 0, K, 0)
+            quantize_w13(e - 1, 0, K, 1)
+            multiply_w13(e - 1, 0, K)
+            round_g(e + 2)
+            round_w2(e + 1)
+            mask_dh(e)
+            make_da(e)
+            quantize_da(e)
+            empty_dx(e - 1, 0, K)
+            quantize_g(e + 1)
+            quantize_w2(e + 1)
+            multiply_w2(e + 1)
+        for kt in range(KT):
+            load_w13(last, kt * P, P)
         for r, pos in enumerate((pos1, pos2, pos3)):
             nc.sync.dma_start(pos_sb[r][:], pos)
-        first_layer(0)
-        load_w2(2)
-        first_layer(1)
-        for e in range(2, E):
-            if e < E - 1:
-                load_w13(e - 2, 0, K)
-            load_a(e)
-            if e < E - 1:
-                load_w2(e + 1)
-            first_layer(e)
-            if e < E - 1:
-                second_layer(e - 2, 0, K)
-        load_w13(WHOLE - 1, 0, K)
-        second_layer(WHOLE - 1, 0, K)
         for kt in range(KT):
-            for e in range(WHOLE, E):
-                load_w13(e, kt * P, P)
-        for kt in range(KT):
-            for e in range(WHOLE, E):
-                second_layer(e, kt * P, P)
-            combine(kt)
+            round_w13(last, kt * P, P)
+            quantize_w13(last, kt * P, P, 0)
+            multiply_w13(last, kt * P, P)
+            empty_dx(last, kt * P, P)
+        for kt in range(KT - 1):
+            for r in range(3):
+                pick(kt, r, 0, T)
+            add_on_tensor(kt, 0, T)
+        for r in range(3):
+            pick(KT - 1, r, 0, T)
+        add(KT - 1, 1, 0)
+        add(KT - 1, 2, 0)
+        store(KT - 1, 0, T, picked[KT - 1, 0, 0])

@@ -20,7 +20,10 @@ P = 128
 PACK = 4
 KT = K // P
 LIST_COLS = C // 16
-AHEAD = 3
+LOADS = [('g', 0), ('l', 0), ('y', 2), ('y', 3), ('y', 0), ('g', 1), ('v', 0), ('g', 2), ('y', 1), ('v', 1), ('a', 0, 1), ('a', 0, 0), ('w', 0, 0, 0, 384), ('g', 3), ('a', 1, 1), ('w', 0, 1, 0, 384), ('g', 4), ('w', 1, 0, 0, 384), ('a', 1, 0), ('v', 2), ('w', 1, 1, 0, 384), ('v', 3), ('a', 2, 0), ('w', 2, 0, 0, 384), ('w', 2, 1, 0, 384), ('g', 5), ('a', 2, 1), ('a', 3, 0), ('v', 4), ('v', 5), ('w', 4, 0, 0, 128), ('a', 3, 1), ('w', 3, 1, 0, 384), ('a', 4, 0), ('w', 3, 0, 0, 384), ('a', 4, 1), ('w', 4, 1, 0, 128), ('w', 5, 0, 256, 128), ('w', 5, 0, 0, 128), ('a', 5, 0), ('a', 5, 1), ('w', 4, 1, 128, 128), ('w', 5, 1, 0, 128), ('w', 5, 1, 128, 128), ('w', 5, 1, 256, 128), ('w', 5, 0, 128, 128), ('l', 1), ('w', 4, 0, 128, 128), ('w', 4, 1, 256, 128), ('w', 4, 0, 256, 128), ('l', 3), ('l', 2)]
+B = {'a': 11, 'w2r': 2, 'g32': 2, 'g16': 2, 'gq': 8, 'w2q': 4, 'w216': 2, 'daq': 2, 'wr384': 3, 'w16_384': 2, 'wq384': 1, 'wr128': 7, 'wr256': 4, 'w16_128': 6, 'w16_256': 10, 'wq128': 7, 'wq256': 3}
+ROUND = ['G', 'rv', 'qg', 'rw', 'A', 'q2', 'ev', 'rg', 'q1']
+PIECES = {-1: [(0, 384)], 0: [(0, 384)], 1: [(0, 384)], 2: [(0, 384)], 3: [(0, 384)], 4: [(0, 128), (128, 128), (256, 128)], 5: [(0, 128), (128, 128), (256, 128)]}
 
 
 def tile_moe_bdx_glu_relu_kernel(
@@ -32,8 +35,8 @@ def tile_moe_bdx_glu_relu_kernel(
         ring = ctx.enter_context(tc.tile_pool(name="ring", bufs=2))
         psum = ctx.enter_context(tc.psum_pool(name="psum", bufs=3))
 
-        offs_sb = keep.tile([P, S // 16], U16, name="offs_sb")
-        pos_sb = [keep.tile([P, T // 16], U16, name="pos_sb%d" % r) for r in range(3)]
+        list_sb = [keep.tile([P, n // 16], U16, name="list_sb%d" % r) for r, n in enumerate((S, T, T, T))]
+        offs_sb, pos_sb = list_sb[0], list_sb[1:]
         dy_sb = [keep.tile([P, T], F32, name="dy_sb%d" % j) for j in range(PACK)]
         gate_sb = [keep.tile([P, C], F32, name="gate_sb%d" % e) for e in range(E)]
         dx_sb = [keep.tile([P, S], F32, name="dx_sb%d" % kt) for kt in range(KT)]
@@ -45,24 +48,27 @@ def tile_moe_bdx_glu_relu_kernel(
         picked, turned, total = {}, {}, {}
 
         def load_w2(e):
-            w2_raw[e] = ring.tile([P, PACK, H], F32, name="w2_raw", bufs=3)
+            w2_raw[e] = ring.tile([P, PACK, H], F32, name="w2_raw", bufs=B["w2r"])
             nc.sync.dma_start(out=w2_raw[e][:], in_=w2[e].rearrange("(p j) i -> p j i", j=PACK))
 
+        def load_list(r):
+            nc.sync.dma_start(list_sb[r][:], (offs, pos1, pos2, pos3)[r])
+
+        def load_dy(j):
+            nc.sync.dma_start(out=dy_sb[j][:], in_=dyT.rearrange("(p j) t -> p j t", j=PACK)[:, j, :])
+
         def load_gate(e):
-            if e < E:
-                nc.sync.dma_start(out=gate_sb[e][:], in_=gate[0:P, e * C : (e + 1) * C])
+            nc.sync.dma_start(out=gate_sb[e][:], in_=gate[0:P, e * C : (e + 1) * C])
 
-        def load_a(e):
-            for w, src in enumerate((a1, a3)):
-                a_raw[e, w] = ring.tile([P, PACK, C], F32, name="a_raw", bufs=10)
-                rows = src.rearrange("(p t) s -> p t s", t=PACK)
-                nc.sync.dma_start(out=a_raw[e, w][:], in_=rows[:, :, e * C : (e + 1) * C])
+        def load_a(e, w):
+            a_raw[e, w] = ring.tile([P, PACK, C], F32, name="a_raw", bufs=B["a"])
+            rows = (a1, a3)[w].rearrange("(p t) s -> p t s", t=PACK)
+            nc.sync.dma_start(out=a_raw[e, w][:], in_=rows[:, :, e * C : (e + 1) * C])
 
-        def load_w13(e, k0, width):
-            for w, src in enumerate((w1, w3)):
-                w13_raw[e, k0, w] = ring.tile([P, PACK, width], F32, name="w13_raw%d" % width, bufs=4 if width == K else 6)
-                rows = src[e].rearrange("(p t) k -> p t k", t=PACK)
-                nc.sync.dma_start(out=w13_raw[e, k0, w][:], in_=rows[:, :, k0 : k0 + width])
+        def load_w13(e, w, k0, width):
+            w13_raw[e, k0, w] = ring.tile([P, PACK, width], F32, name="w13_raw%d" % width, bufs=B["wr%d" % width])
+            rows = (w1, w3)[w][e].rearrange("(p t) k -> p t k", t=PACK)
+            nc.sync.dma_start(out=w13_raw[e, k0, w][:], in_=rows[:, :, k0 : k0 + width])
 
         def mx_tiles(words, name, bufs):
             codes = ring.tile([P, words], U32, name=name + "_codes", bufs=bufs, align_bytes=64)
@@ -95,26 +101,26 @@ def tile_moe_bdx_glu_relu_kernel(
             if e >= E:
                 return
             if j == 0:
-                g32[e] = ring.tile([P, PACK, C], F32, name="g32", bufs=2)
+                g32[e] = ring.tile([P, PACK, C], F32, name="g32", bufs=B["g32"])
             window = dy_sb[j][:].indirect(offs_sb[:, e * LIST_COLS : (e + 1) * LIST_COLS])
             nc.vector.tensor_tensor(g32[e][:, j, :], window, gate_sb[e][:], ALU.mult)
 
         def round_g(e):
             if e >= E:
                 return
-            g16[e] = ring.tile([P, PACK * C], BF16, name="g16", bufs=2, align_bytes=64)
+            g16[e] = ring.tile([P, PACK * C], BF16, name="g16", bufs=B["g16"], align_bytes=64)
             nc.scalar.copy(out=words_by_four(g16[e][:]), in_=rows_by_four(g32[e][:]))
 
         def quantize_g(e):
             if e >= E:
                 return
-            g_q[e] = mx_tiles(C, "g", 2)
+            g_q[e] = mx_tiles(C, "g", B["gq"])
             quantize(g_q[e], g16[e], 0, C)
 
         def round_w2(e):
             if e >= E:
                 return
-            w2_16[e] = ring.tile([P, PACK * H], BF16, name="w2_16", bufs=2, align_bytes=64)
+            w2_16[e] = ring.tile([P, PACK * H], BF16, name="w2_16", bufs=B["w216"], align_bytes=64)
             nc.scalar.copy(
                 out=w2_16[e][:].rearrange("p (t m j) -> p m j t", t=PACK, j=PACK),
                 in_=w2_raw[e][:].rearrange("p j (m t) -> p m j t", t=PACK),
@@ -123,7 +129,7 @@ def tile_moe_bdx_glu_relu_kernel(
         def quantize_w2(e):
             if e >= E:
                 return
-            w2_q[e] = mx_tiles(H, "w2", 2)
+            w2_q[e] = mx_tiles(H, "w2", B["w2q"])
             quantize(w2_q[e], w2_16[e], 0, H)
 
         def multiply_w2(e):
@@ -152,21 +158,21 @@ def tile_moe_bdx_glu_relu_kernel(
                 for half in range(2):
                     lo = PACK * (w * C + half * P)
                     nc.vector.tensor_tensor(
-                        words_by_four(da16[e][:, lo : lo + PACK * P]),
-                        rows_by_four(live[e, half][:]),
-                        rows_by_four(a_raw[e, 1 - w][:, :, half * P : (half + 1) * P]),
+                        da16[e][:, lo : lo + PACK * P].rearrange("p (c i t) -> p c t i", i=2, t=PACK),
+                        live[e, half][:].rearrange("p t (c i) -> p c t i", i=2),
+                        a_raw[e, 1 - w][:, :, half * P : (half + 1) * P].rearrange("p t (c i) -> p c t i", i=2),
                         ALU.mult,
                     )
 
         def quantize_da(e):
-            da_q[e] = mx_tiles(2 * C, "da", 3)
+            da_q[e] = mx_tiles(2 * C, "da", B["daq"])
             for w in (1, 0):
                 quantize(da_q[e], da16[e], w * C, (w + 1) * C)
 
         def round_w13(e, k0, width):
             if e < 0:
                 return
-            w13_16[e, k0] = ring.tile([P, 2 * PACK * width], BF16, name="w13_16_%d" % width, bufs=2 if width == K else 3, align_bytes=64)
+            w13_16[e, k0] = ring.tile([P, 2 * PACK * width], BF16, name="w13_16_%d" % width, bufs=B["w16_%d" % width], align_bytes=64)
             for w in range(2):
                 nc.scalar.copy(
                     out=words_by_four(w13_16[e, k0][:, w * PACK * width : (w + 1) * PACK * width]),
@@ -177,7 +183,7 @@ def tile_moe_bdx_glu_relu_kernel(
             if e < 0:
                 return
             if part == 0:
-                w13_q[e, k0] = mx_tiles(2 * width, "w13_%d" % width, 2 if width == K else 3)
+                w13_q[e, k0] = mx_tiles(2 * width, "w13_%d" % width, B["wq%d" % width])
             lo, hi = ((0, 512), (512, 768))[part] if width == K else (0, 2 * width)
             quantize(w13_q[e, k0], w13_16[e, k0], lo, hi)
 
@@ -185,19 +191,20 @@ def tile_moe_bdx_glu_relu_kernel(
             if e < 0:
                 return
             for k in range(0, width, P):
-                dx[e, k0 + k] = psum.tile([P, C], F32, name="dx", bufs=4)
+                if e % 2 == 0:
+                    dx[e // 2, k0 + k] = psum.tile([P, 2, C], F32, name="dx", bufs=6)
                 for w in range(2):
                     cols = slice(w * width + k, w * width + k + P)
-                    product(dx[e, k0 + k][:], w13_q[e, k0], cols, da_q[e], slice(w * C, (w + 1) * C), w == 0, w == 1)
+                    product(dx[e // 2, k0 + k][:, e % 2, :], w13_q[e, k0], cols, da_q[e], slice(w * C, (w + 1) * C), w == 0, w == 1)
 
         def empty_dx(e, k0, width):
-            if e < 0:
+            if e < 0 or e % 2 == 0:
                 return
             for k in range(k0, k0 + width, P):
-                nc.scalar.copy(out=dx_sb[k // P][:, e * C : (e + 1) * C], in_=dx[e, k][:])
+                nc.scalar.copy(out=dx_sb[k // P][:, (e - 1) * C : (e + 1) * C], in_=dx[e // 2, k][:].rearrange("p u c -> p (u c)"))
 
         def pick(kt, r, lo, hi):
-            picked[kt, r, lo] = ring.tile([P, hi - lo], F32, name="a_raw", bufs=10)
+            picked[kt, r, lo] = ring.tile([P, hi - lo], F32, name="a_raw", bufs=B["a"])
             nc.vector.tensor_copy(picked[kt, r, lo][:], dx_sb[kt][:].indirect(pos_sb[r][:, lo // 16 : hi // 16]))
 
         def add(kt, r, lo):
@@ -224,15 +231,9 @@ def tile_moe_bdx_glu_relu_kernel(
             nc.scalar.copy(out=result[:], in_=back[:])
             nc.scalar.dma_start(out=out[kt * P : (kt + 1) * P, lo:hi].rearrange("p (b t) -> p b t", t=P), in_=result[:])
 
-        dy_rows = dyT.rearrange("(p j) t -> p j t", j=PACK)
-        nc.sync.dma_start(offs_sb[:], offs)
-        load_gate(0)
-        nc.sync.dma_start(out=dy_sb[0][:], in_=dy_rows[:, 0, :])
-        load_gate(1)
-        for j in range(1, PACK):
-            if j == PACK - 1:
-                load_w2(0)
-            nc.sync.dma_start(out=dy_sb[j][:], in_=dy_rows[:, j, :])
+        loaders = {"l": load_list, "y": load_dy, "g": load_gate, "v": load_w2, "a": load_a, "w": load_w13}
+        for step in LOADS:
+            loaders[step[0]](*step[1:])
         for j in range(PACK):
             for e in range(2):
                 gather_g(e, j)
@@ -243,43 +244,56 @@ def tile_moe_bdx_glu_relu_kernel(
         multiply_w2(0)
         round_g(1)
         last = E - 1
-        for e in range(E):
-            if e > 0:
-                load_w13(e - 1, 0, K)
-            load_gate(e + 2)
-            if e < last:
-                load_w2(e + 1)
-            load_a(e)
-            round_w13(e - 1, 0, K)
+
+        def gathers(e):
             for j in range(PACK):
-                gather_g(e + 2, j)
-            quantize_w13(e - 1, 0, K, 0)
-            quantize_w13(e - 1, 0, K, 1)
-            multiply_w13(e - 1, 0, K)
-            round_g(e + 2)
-            round_w2(e + 1)
+                gather_g(e, j)
+
+        def second(e):
+            width = PIECES[e][0][1] if e >= 0 else K
+            quantize_w13(e, 0, width, 0)
+            if width == K:
+                quantize_w13(e, 0, width, 1)
+            multiply_w13(e, 0, width)
+
+        def middle(e):
             mask_dh(e)
             make_da(e)
             quantize_da(e)
-            empty_dx(e - 1, 0, K)
-            quantize_g(e + 1)
-            quantize_w2(e + 1)
-            multiply_w2(e + 1)
+
+        def first(e):
+            quantize_w2(e)
+            multiply_w2(e)
+
+        for e in range(E):
+            todo = {
+                "rw": lambda: round_w13(e - 1, 0, PIECES[e - 1][0][1]), "G": lambda: gathers(e + 2), "q2": lambda: second(e - 1),
+                "rg": lambda: round_g(e + 2), "rv": lambda: round_w2(e + 1), "A": lambda: middle(e),
+                "ev": lambda: empty_dx(e - 1, 0, K), "qg": lambda: quantize_g(e + 1), "q1": lambda: first(e + 1),
+            }
+            for name in ROUND:
+                todo[name]()
         for kt in range(KT):
-            load_w13(last, kt * P, P)
-        for r, pos in enumerate((pos1, pos2, pos3)):
-            nc.sync.dma_start(pos_sb[r][:], pos)
-        for kt in range(KT):
-            round_w13(last, kt * P, P)
-            quantize_w13(last, kt * P, P, 0)
-            multiply_w13(last, kt * P, P)
+            for e in (last - 1, last):
+                for k0, width in PIECES[e]:
+                    if k0 == kt * P and (e == last or k0 > 0):
+                        round_w13(e, k0, width)
+                        quantize_w13(e, k0, width, 0)
+                        multiply_w13(e, k0, width)
             empty_dx(last, kt * P, P)
         for kt in range(KT - 1):
             for r in range(3):
                 pick(kt, r, 0, T)
             add_on_tensor(kt, 0, T)
+        kt, half = KT - 1, T // 2
         for r in range(3):
-            pick(KT - 1, r, 0, T)
-        add(KT - 1, 1, 0)
-        add(KT - 1, 2, 0)
-        store(KT - 1, 0, T, picked[KT - 1, 0, 0])
+            pick(kt, r, 0, half)
+        add(kt, 1, 0)
+        pick(kt, 0, half, T)
+        add(kt, 2, 0)
+        store(kt, 0, half, picked[kt, 0, 0])
+        pick(kt, 1, half, T)
+        pick(kt, 2, half, T)
+        add(kt, 1, half)
+        add(kt, 2, half)
+        store(kt, half, T, picked[kt, 0, half])

@@ -20,10 +20,12 @@ P = 128
 PACK = 4
 KT = K // P
 LIST_COLS = C // 16
-LOADS = [('g', 0), ('l', 0), ('y', 2), ('y', 3), ('y', 0), ('g', 1), ('v', 0), ('g', 2), ('y', 1), ('v', 1), ('a', 0, 1), ('a', 0, 0), ('w', 0, 0, 0, 384), ('g', 3), ('a', 1, 1), ('w', 0, 1, 0, 384), ('g', 4), ('w', 1, 0, 0, 384), ('a', 1, 0), ('v', 2), ('w', 1, 1, 0, 384), ('v', 3), ('a', 2, 0), ('w', 2, 0, 0, 384), ('w', 2, 1, 0, 384), ('g', 5), ('a', 2, 1), ('a', 3, 0), ('v', 4), ('v', 5), ('w', 4, 0, 0, 128), ('a', 3, 1), ('w', 3, 1, 0, 384), ('a', 4, 0), ('w', 3, 0, 0, 384), ('a', 4, 1), ('w', 4, 1, 0, 128), ('w', 5, 0, 256, 128), ('w', 5, 0, 0, 128), ('a', 5, 0), ('a', 5, 1), ('w', 4, 1, 128, 128), ('w', 5, 1, 0, 128), ('w', 5, 1, 128, 128), ('w', 5, 1, 256, 128), ('w', 5, 0, 128, 128), ('l', 1), ('w', 4, 0, 128, 128), ('w', 4, 1, 256, 128), ('w', 4, 0, 256, 128), ('l', 3), ('l', 2)]
-B = {'a': 11, 'w2r': 2, 'g32': 2, 'g16': 2, 'gq': 8, 'w2q': 4, 'w216': 2, 'daq': 2, 'wr384': 3, 'w16_384': 2, 'wq384': 1, 'wr128': 7, 'wr256': 4, 'w16_128': 6, 'w16_256': 10, 'wq128': 7, 'wq256': 3}
-ROUND = ['G', 'rv', 'qg', 'rw', 'A', 'q2', 'ev', 'rg', 'q1']
+LOADS = [('y', 0), ('l', 0), ('g', 0), ('g', 1), ('y', 2), ('y', 3), ('g', 2), ('v', 0, 0, 256), ('v', 0, 256, 512), ('g', 3), ('y', 1), ('g', 4), ('v', 1, 0, 512), ('w', 0, 0, 0, 384), ('w', 0, 1, 0, 384), ('a', 0, 0), ('a', 0, 1), ('w', 1, 0, 0, 384), ('a', 1, 0), ('w', 1, 1, 0, 384), ('v', 2, 0, 512), ('a', 1, 1), ('v', 3, 0, 512), ('g', 5), ('w', 2, 0, 0, 384), ('a', 2, 1), ('a', 2, 0), ('a', 3, 0), ('v', 4, 0, 512), ('w', 2, 1, 0, 384), ('w', 4, 1, 0, 128), ('a', 3, 1), ('v', 5, 0, 512), ('a', 4, 0), ('w', 3, 1, 0, 384), ('w', 3, 0, 0, 384), ('a', 4, 1), ('w', 4, 0, 0, 128), ('w', 5, 0, 0, 128), ('a', 5, 0), ('w', 5, 1, 0, 128), ('a', 5, 1), ('w', 5, 0, 256, 128), ('w', 5, 1, 256, 128), ('w', 5, 1, 128, 128), ('w', 5, 0, 128, 128), ('w', 4, 0, 128, 128), ('l', 1), ('w', 4, 1, 128, 128), ('w', 4, 1, 256, 128), ('l', 2), ('w', 4, 0, 256, 128), ('l', 3)]
+B = {'a': 5, 'w2r': 3, 'g32': 3, 'g16': 2, 'gq': 6, 'w2q': 3, 'w216': 1, 'daq': 3, 'wr384': 4, 'w16_384': 3, 'wq384': 3, 'wr128': 10, 'wr256': 5, 'w16_128': 6, 'w16_256': 7, 'wq128': 5, 'wq256': 1}
+ROUND = ['A', 'rv', 'rw', 'G', 'q2', 'rg', 'qg', 'ev', 'q1']
 PIECES = {-1: [(0, 384)], 0: [(0, 384)], 1: [(0, 384)], 2: [(0, 384)], 3: [(0, 384)], 4: [(0, 128), (128, 128), (256, 128)], 5: [(0, 128), (128, 128), (256, 128)]}
+SPLIT = 1
+TAIL = [('p', 5, 0), ('e', 0), ('p', 5, 2), ('p', 5, 1), ('p', 4, 1), ('k', 0, 0), ('e', 1), ('p', 4, 2), ('k', 0, 1), ('k', 0, 2), ('s', 0), ('k', 1, 0), ('k', 1, 2), ('k', 1, 1), ('e', 2), ('s', 1)]
 
 
 def tile_moe_bdx_glu_relu_kernel(
@@ -47,9 +49,9 @@ def tile_moe_bdx_glu_relu_kernel(
         g32, g16, g_q, w2_16, w2_q, dh, live, da16, da_q, w13_16, w13_q, dx = ({} for i in range(12))
         picked, turned, total = {}, {}, {}
 
-        def load_w2(e):
-            w2_raw[e] = ring.tile([P, PACK, H], F32, name="w2_raw", bufs=B["w2r"])
-            nc.sync.dma_start(out=w2_raw[e][:], in_=w2[e].rearrange("(p j) i -> p j i", j=PACK))
+        def load_w2(e, lo, hi):
+            w2_raw[e, lo] = ring.tile([P, PACK, hi - lo], F32, name="w2_raw", bufs=B["w2r"])
+            nc.sync.dma_start(out=w2_raw[e, lo][:], in_=w2[e].rearrange("(p j) i -> p j i", j=PACK)[:, :, lo:hi])
 
         def load_list(r):
             nc.sync.dma_start(list_sb[r][:], (offs, pos1, pos2, pos3)[r])
@@ -120,17 +122,18 @@ def tile_moe_bdx_glu_relu_kernel(
         def round_w2(e):
             if e >= E:
                 return
-            w2_16[e] = ring.tile([P, PACK * H], BF16, name="w2_16", bufs=B["w216"], align_bytes=64)
-            nc.scalar.copy(
-                out=w2_16[e][:].rearrange("p (t m j) -> p m j t", t=PACK, j=PACK),
-                in_=w2_raw[e][:].rearrange("p j (m t) -> p m j t", t=PACK),
-            )
+            w2_16[e] = ring.tile([P, PACK, P * PACK], BF16, name="w2_16", bufs=B["w216"], align_bytes=64)
+            for lo, hi in ((0, H // 2), (H // 2, H)) if e < SPLIT else ((0, H),):
+                nc.scalar.copy(
+                    out=w2_16[e][:, :, lo:hi].rearrange("p t (m j) -> p m j t", j=PACK),
+                    in_=w2_raw[e, lo][:].rearrange("p j (m t) -> p m j t", t=PACK),
+                )
 
         def quantize_w2(e):
             if e >= E:
                 return
             w2_q[e] = mx_tiles(H, "w2", B["w2q"])
-            quantize(w2_q[e], w2_16[e], 0, H)
+            quantize(w2_q[e], w2_16[e][:].rearrange("p t x -> p (t x)"), 0, H)
 
         def multiply_w2(e):
             if e >= E:
@@ -191,7 +194,7 @@ def tile_moe_bdx_glu_relu_kernel(
             if e < 0:
                 return
             for k in range(0, width, P):
-                if e % 2 == 0:
+                if (e // 2, k0 + k) not in dx:
                     dx[e // 2, k0 + k] = psum.tile([P, 2, C], F32, name="dx", bufs=6)
                 for w in range(2):
                     cols = slice(w * width + k, w * width + k + P)
@@ -215,15 +218,16 @@ def tile_moe_bdx_glu_relu_kernel(
 
         def add_on_tensor(kt, lo, hi):
             blocks = (hi - lo) // P
-            summed = psum.tile([P, blocks, P], F32, name="dh", bufs=2)
-            for b in range(blocks):
-                for r in range(3):
+            summed = [psum.tile([P, P], F32, name="dx", bufs=6) for b in range(blocks)]
+            for r in range(3):
+                for b in range(blocks):
                     nc.tensor.matmul(
-                        summed[:, b, :], picked[kt, r, lo][:, b * P : (b + 1) * P], ident[:],
+                        summed[b][:], picked[kt, r, lo][:, b * P : (b + 1) * P], ident[:],
                         start=(r == 0), stop=(r == 2), is_transpose=True,
                     )
             turned = ring.tile([P, blocks, P], F32, name="turned", bufs=2)
-            nc.scalar.copy(out=turned[:], in_=summed[:])
+            for b in range(blocks):
+                nc.scalar.copy(out=turned[:, b, :], in_=summed[b][:])
             back = psum.tile([P, blocks, P], F32, name="dh", bufs=2)
             for b in range(blocks):
                 nc.tensor.transpose(back[:, b, :], turned[:, b, :], ident[:])
@@ -235,7 +239,7 @@ def tile_moe_bdx_glu_relu_kernel(
         for step in LOADS:
             loaders[step[0]](*step[1:])
         for j in range(PACK):
-            for e in range(2):
+            for e in range(3):
                 gather_g(e, j)
         round_w2(0)
         round_g(0)
@@ -267,24 +271,23 @@ def tile_moe_bdx_glu_relu_kernel(
 
         for e in range(E):
             todo = {
-                "rw": lambda: round_w13(e - 1, 0, PIECES[e - 1][0][1]), "G": lambda: gathers(e + 2), "q2": lambda: second(e - 1),
+                "rw": lambda: round_w13(e - 1, 0, PIECES[e - 1][0][1]), "G": lambda: gathers(e + 2 if e else E), "q2": lambda: second(e - 1),
                 "rg": lambda: round_g(e + 2), "rv": lambda: round_w2(e + 1), "A": lambda: middle(e),
                 "ev": lambda: empty_dx(e - 1, 0, K), "qg": lambda: quantize_g(e + 1), "q1": lambda: first(e + 1),
             }
             for name in ROUND:
                 todo[name]()
-        for kt in range(KT):
-            for e in (last - 1, last):
-                for k0, width in PIECES[e]:
-                    if k0 == kt * P and (e == last or k0 > 0):
-                        round_w13(e, k0, width)
-                        quantize_w13(e, k0, width, 0)
-                        multiply_w13(e, k0, width)
-            empty_dx(last, kt * P, P)
-        for kt in range(KT - 1):
-            for r in range(3):
-                pick(kt, r, 0, T)
-            add_on_tensor(kt, 0, T)
+        def piece(e, kt):
+            round_w13(e, kt * P, P)
+            quantize_w13(e, kt * P, P, 0)
+            multiply_w13(e, kt * P, P)
+
+        ending = {
+            "p": piece, "e": lambda kt: empty_dx(last, kt * P, P), "k": lambda kt, r: pick(kt, r, 0, T),
+            "s": lambda kt: add_on_tensor(kt, 0, T),
+        }
+        for step in TAIL:
+            ending[step[0]](*step[1:])
         kt, half = KT - 1, T // 2
         for r in range(3):
             pick(kt, r, 0, half)

from contextlib import ExitStack

import concourse.mybir as mybir
from concourse.masks import make_identity

K, T, E, C, H, N = 384, 512, 6, 256, 512, 512
S = E * C
FLOPS = 2 * S * (N * H + 2 * H * K)
BYTES = 4 * (N * T + 2 * H * S + E * N * H + 2 * E * H * K + 128 * S + K * T) + 2 * 128 * (S + 3 * T) // 16

F32 = mybir.dt.float32
BF16 = mybir.dt.bfloat16
U32 = mybir.dt.uint32
U16 = mybir.dt.uint16
U8 = mybir.dt.uint8
FP8X4 = mybir.dt.float8_e4m3fn_x4
ALU = mybir.AluOpType

P = 128
PACK = 4
KT = K // P
LIST_COLS = C // 16
LOADS = [('y', 0), ('l', 0), ('g', 0), ('g', 1), ('y', 2), ('y', 3), ('g', 2), ('v', 0, 0, 256), ('v', 0, 256, 512), ('g', 3), ('y', 1), ('g', 4), ('v', 1, 0, 512), ('w', 0, 0, 0, 384), ('w', 0, 1, 0, 384), ('a', 0, 0), ('a', 0, 1), ('w', 1, 0, 0, 384), ('a', 1, 0), ('w', 1, 1, 0, 384), ('v', 2, 0, 512), ('a', 1, 1), ('v', 3, 0, 512), ('g', 5), ('w', 2, 0, 0, 384), ('a', 2, 1), ('a', 2, 0), ('a', 3, 0), ('v', 4, 0, 512), ('w', 2, 1, 0, 384), ('w', 4, 1, 0, 128), ('a', 3, 1), ('v', 5, 0, 512), ('a', 4, 0), ('w', 3, 1, 0, 384), ('w', 3, 0, 0, 384), ('a', 4, 1), ('w', 4, 0, 0, 128), ('w', 5, 0, 0, 128), ('a', 5, 0), ('w', 5, 1, 0, 128), ('a', 5, 1), ('w', 5, 0, 256, 128), ('w', 5, 1, 256, 128), ('w', 5, 1, 128, 128), ('w', 5, 0, 128, 128), ('w', 4, 0, 128, 128), ('l', 1), ('w', 4, 1, 128, 128), ('w', 4, 1, 256, 128), ('l', 2), ('w', 4, 0, 256, 128), ('l', 3)]
B = {'a': 5, 'w2r': 3, 'g32': 3, 'g16': 2, 'gq': 6, 'w2q': 3, 'w216': 1, 'daq': 3, 'wr384': 4, 'w16_384': 3, 'wq384': 3, 'wr128': 10, 'wr256': 5, 'w16_128': 6, 'w16_256': 7, 'wq128': 5, 'wq256': 1}
ROUND = ['A', 'rv', 'rw', 'G', 'q2', 'rg', 'qg', 'ev', 'q1']
PIECES = {-1: [(0, 384)], 0: [(0, 384)], 1: [(0, 384)], 2: [(0, 384)], 3: [(0, 384)], 4: [(0, 128), (128, 128), (256, 128)], 5: [(0, 128), (128, 128), (256, 128)]}
SPLIT = 1
TAIL = [('p', 5, 0), ('e', 0), ('p', 5, 2), ('p', 5, 1), ('p', 4, 1), ('k', 0, 0), ('e', 1), ('p', 4, 2), ('k', 0, 1), ('k', 0, 2), ('s', 0), ('k', 1, 0), ('k', 1, 2), ('k', 1, 1), ('e', 2), ('s', 1)]


def tile_moe_bdx_glu_relu_kernel(
    tc, dyT, a1, a3, w2, w1, w3, gate, offs, pos1, pos2, pos3, out
):
    nc = tc.nc
    with ExitStack() as ctx:
        keep = ctx.enter_context(tc.tile_pool(name="keep", bufs=1))
        ring = ctx.enter_context(tc.tile_pool(name="ring", bufs=2))
        psum = ctx.enter_context(tc.psum_pool(name="psum", bufs=3))

        list_sb = [keep.tile([P, n // 16], U16, name="list_sb%d" % r) for r, n in enumerate((S, T, T, T))]
        offs_sb, pos_sb = list_sb[0], list_sb[1:]
        dy_sb = [keep.tile([P, T], F32, name="dy_sb%d" % j) for j in range(PACK)]
        gate_sb = [keep.tile([P, C], F32, name="gate_sb%d" % e) for e in range(E)]
        dx_sb = [keep.tile([P, S], F32, name="dx_sb%d" % kt) for kt in range(KT)]
        ident = keep.tile([P, P], F32, name="ident")
        make_identity(nc, ident[:])

        w2_raw, a_raw, w13_raw = {}, {}, {}
        g32, g16, g_q, w2_16, w2_q, dh, live, da16, da_q, w13_16, w13_q, dx = ({} for i in range(12))
        picked, turned, total = {}, {}, {}

        def load_w2(e, lo, hi):
            w2_raw[e, lo] = ring.tile([P, PACK, hi - lo], F32, name="w2_raw", bufs=B["w2r"])
            nc.sync.dma_start(out=w2_raw[e, lo][:], in_=w2[e].rearrange("(p j) i -> p j i", j=PACK)[:, :, lo:hi])

        def load_list(r):
            nc.sync.dma_start(list_sb[r][:], (offs, pos1, pos2, pos3)[r])

        def load_dy(j):
            nc.sync.dma_start(out=dy_sb[j][:], in_=dyT.rearrange("(p j) t -> p j t", j=PACK)[:, j, :])

        def load_gate(e):
            nc.sync.dma_start(out=gate_sb[e][:], in_=gate[0:P, e * C : (e + 1) * C])

        def load_a(e, w):
            a_raw[e, w] = ring.tile([P, PACK, C], F32, name="a_raw", bufs=B["a"])
            rows = (a1, a3)[w].rearrange("(p t) s -> p t s", t=PACK)
            nc.sync.dma_start(out=a_raw[e, w][:], in_=rows[:, :, e * C : (e + 1) * C])

        def load_w13(e, w, k0, width):
            w13_raw[e, k0, w] = ring.tile([P, PACK, width], F32, name="w13_raw%d" % width, bufs=B["wr%d" % width])
            rows = (w1, w3)[w][e].rearrange("(p t) k -> p t k", t=PACK)
            nc.sync.dma_start(out=w13_raw[e, k0, w][:], in_=rows[:, :, k0 : k0 + width])

        def mx_tiles(words, name, bufs):
            codes = ring.tile([P, words], U32, name=name + "_codes", bufs=bufs, align_bytes=64)
            scales = ring.tile([P, words], U8, name=name + "_scales", bufs=bufs, align_bytes=64)
            return codes, scales

        def quantize(pair, grouped, lo, hi):
            nc.vector.quantize_mx(
                out=pair[0][:, lo:hi].bitcast(FP8X4), scales=pair[1][:, lo:hi], in_=grouped[:, PACK * lo : PACK * hi]
            )

        def product(dst, left, cols, right, slots, start, stop):
            nc.tensor.matmul_mx(
                out=dst,
                lhsT=left[0][:, cols].bitcast(FP8X4),
                lhsT_scale=left[1][:, cols],
                rhs=right[0][:, slots].bitcast(FP8X4),
                rhs_scale=right[1][:, slots],
                start=start,
                stop=stop,
            )

        def rows_by_four(ap):
            return ap.rearrange("p t (c i) -> p c t i", i=4)

        def words_by_four(ap):
            return ap.rearrange("p (c i t) -> p c t i", i=4, t=PACK)

        def gather_g(e, j):
            if e >= E:
                return
            if j == 0:
                g32[e] = ring.tile([P, PACK, C], F32, name="g32", bufs=B["g32"])
            window = dy_sb[j][:].indirect(offs_sb[:, e * LIST_COLS : (e + 1) * LIST_COLS])
            nc.vector.tensor_tensor(g32[e][:, j, :], window, gate_sb[e][:], ALU.mult)

        def round_g(e):
            if e >= E:
                return
            g16[e] = ring.tile([P, PACK * C], BF16, name="g16", bufs=B["g16"], align_bytes=64)
            nc.scalar.copy(out=words_by_four(g16[e][:]), in_=rows_by_four(g32[e][:]))

        def quantize_g(e):
            if e >= E:
                return
            g_q[e] = mx_tiles(C, "g", B["gq"])
            quantize(g_q[e], g16[e], 0, C)

        def round_w2(e):
            if e >= E:
                return
            w2_16[e] = ring.tile([P, PACK, P * PACK], BF16, name="w2_16", bufs=B["w216"], align_bytes=64)
            for lo, hi in ((0, H // 2), (H // 2, H)) if e < SPLIT else ((0, H),):
                nc.scalar.copy(
                    out=w2_16[e][:, :, lo:hi].rearrange("p t (m j) -> p m j t", j=PACK),
                    in_=w2_raw[e, lo][:].rearrange("p j (m t) -> p m j t", t=PACK),
                )

        def quantize_w2(e):
            if e >= E:
                return
            w2_q[e] = mx_tiles(H, "w2", B["w2q"])
            quantize(w2_q[e], w2_16[e][:].rearrange("p t x -> p (t x)"), 0, H)

        def multiply_w2(e):
            if e >= E:
                return
            for half in range(2):
                dh[e, half] = psum.tile([P, PACK, P], F32, name="dh", bufs=2)
                for t in range(PACK):
                    product(dh[e, half][:, t, :], w2_q[e], slice(t * P, (t + 1) * P), g_q[e], slice(half * P, (half + 1) * P), True, True)

        def mask_dh(e):
            for half in range(2):
                live[e, half] = ring.tile([P, PACK, P], F32, name="live", bufs=2)
                nc.vector.scalar_tensor_tensor(
                    out=live[e, half][:],
                    in0=a_raw[e, 0][:, :, half * P : (half + 1) * P],
                    scalar=0.0,
                    in1=dh[e, half][:],
                    op0=ALU.is_gt,
                    op1=ALU.mult,
                )

        def make_da(e):
            da16[e] = ring.tile([P, 2 * PACK * C], BF16, name="da16", bufs=1, align_bytes=64)
            for w in (1, 0):
                for half in range(2):
                    lo = PACK * (w * C + half * P)
                    nc.vector.tensor_tensor(
                        da16[e][:, lo : lo + PACK * P].rearrange("p (c i t) -> p c t i", i=2, t=PACK),
                        live[e, half][:].rearrange("p t (c i) -> p c t i", i=2),
                        a_raw[e, 1 - w][:, :, half * P : (half + 1) * P].rearrange("p t (c i) -> p c t i", i=2),
                        ALU.mult,
                    )

        def quantize_da(e):
            da_q[e] = mx_tiles(2 * C, "da", B["daq"])
            for w in (1, 0):
                quantize(da_q[e], da16[e], w * C, (w + 1) * C)

        def round_w13(e, k0, width):
            if e < 0:
                return
            w13_16[e, k0] = ring.tile([P, 2 * PACK * width], BF16, name="w13_16_%d" % width, bufs=B["w16_%d" % width], align_bytes=64)
            for w in range(2):
                nc.scalar.copy(
                    out=words_by_four(w13_16[e, k0][:, w * PACK * width : (w + 1) * PACK * width]),
                    in_=rows_by_four(w13_raw[e, k0, w][:]),
                )

        def quantize_w13(e, k0, width, part):
            if e < 0:
                return
            if part == 0:
                w13_q[e, k0] = mx_tiles(2 * width, "w13_%d" % width, B["wq%d" % width])
            lo, hi = ((0, 512), (512, 768))[part] if width == K else (0, 2 * width)
            quantize(w13_q[e, k0], w13_16[e, k0], lo, hi)

        def multiply_w13(e, k0, width):
            if e < 0:
                return
            for k in range(0, width, P):
                if (e // 2, k0 + k) not in dx:
                    dx[e // 2, k0 + k] = psum.tile([P, 2, C], F32, name="dx", bufs=6)
                for w in range(2):
                    cols = slice(w * width + k, w * width + k + P)
                    product(dx[e // 2, k0 + k][:, e % 2, :], w13_q[e, k0], cols, da_q[e], slice(w * C, (w + 1) * C), w == 0, w == 1)

        def empty_dx(e, k0, width):
            if e < 0 or e % 2 == 0:
                return
            for k in range(k0, k0 + width, P):
                nc.scalar.copy(out=dx_sb[k // P][:, (e - 1) * C : (e + 1) * C], in_=dx[e // 2, k][:].rearrange("p u c -> p (u c)"))

        def pick(kt, r, lo, hi):
            picked[kt, r, lo] = ring.tile([P, hi - lo], F32, name="a_raw", bufs=B["a"])
            nc.vector.tensor_copy(picked[kt, r, lo][:], dx_sb[kt][:].indirect(pos_sb[r][:, lo // 16 : hi // 16]))

        def add(kt, r, lo):
            nc.vector.tensor_tensor(picked[kt, 0, lo][:], picked[kt, 0, lo][:], picked[kt, r, lo][:], ALU.add)

        def store(kt, lo, hi, src):
            nc.sync.dma_start(out=out[kt * P : (kt + 1) * P, lo:hi], in_=src[:])

        def add_on_tensor(kt, lo, hi):
            blocks = (hi - lo) // P
            summed = [psum.tile([P, P], F32, name="dx", bufs=6) for b in range(blocks)]
            for r in range(3):
                for b in range(blocks):
                    nc.tensor.matmul(
                        summed[b][:], picked[kt, r, lo][:, b * P : (b + 1) * P], ident[:],
                        start=(r == 0), stop=(r == 2), is_transpose=True,
                    )
            turned = ring.tile([P, blocks, P], F32, name="turned", bufs=2)
            for b in range(blocks):
                nc.scalar.copy(out=turned[:, b, :], in_=summed[b][:])
            back = psum.tile([P, blocks, P], F32, name="dh", bufs=2)
            for b in range(blocks):
                nc.tensor.transpose(back[:, b, :], turned[:, b, :], ident[:])
            result = ring.tile([P, blocks, P], F32, name="result", bufs=2)
            nc.scalar.copy(out=result[:], in_=back[:])
            nc.scalar.dma_start(out=out[kt * P : (kt + 1) * P, lo:hi].rearrange("p (b t) -> p b t", t=P), in_=result[:])

        loaders = {"l": load_list, "y": load_dy, "g": load_gate, "v": load_w2, "a": load_a, "w": load_w13}
        for step in LOADS:
            loaders[step[0]](*step[1:])
        for j in range(PACK):
            for e in range(3):
                gather_g(e, j)
        round_w2(0)
        round_g(0)
        quantize_w2(0)
        quantize_g(0)
        multiply_w2(0)
        round_g(1)
        last = E - 1

        def gathers(e):
            for j in range(PACK):
                gather_g(e, j)

        def second(e):
            width = PIECES[e][0][1] if e >= 0 else K
            quantize_w13(e, 0, width, 0)
            if width == K:
                quantize_w13(e, 0, width, 1)
            multiply_w13(e, 0, width)

        def middle(e):
            mask_dh(e)
            make_da(e)
            quantize_da(e)

        def first(e):
            quantize_w2(e)
            multiply_w2(e)

        for e in range(E):
            todo = {
                "rw": lambda: round_w13(e - 1, 0, PIECES[e - 1][0][1]), "G": lambda: gathers(e + 2 if e else E), "q2": lambda: second(e - 1),
                "rg": lambda: round_g(e + 2), "rv": lambda: round_w2(e + 1), "A": lambda: middle(e),
                "ev": lambda: empty_dx(e - 1, 0, K), "qg": lambda: quantize_g(e + 1), "q1": lambda: first(e + 1),
            }
            for name in ROUND:
                todo[name]()
        def piece(e, kt):
            round_w13(e, kt * P, P)
            quantize_w13(e, kt * P, P, 0)
            multiply_w13(e, kt * P, P)

        ending = {
            "p": piece, "e": lambda kt: empty_dx(last, kt * P, P), "k": lambda kt, r: pick(kt, r, 0, T),
            "s": lambda kt: add_on_tensor(kt, 0, T),
        }
        for step in TAIL:
            ending[step[0]](*step[1:])
        kt, half = KT - 1, T // 2
        for r in range(3):
            pick(kt, r, 0, half)
        add(kt, 1, 0)
        pick(kt, 0, half, T)
        add(kt, 2, 0)
        store(kt, 0, half, picked[kt, 0, 0])
        pick(kt, 1, half, T)
        pick(kt, 2, half, T)
        add(kt, 1, half)
        add(kt, 2, half)
        store(kt, half, T, picked[kt, 0, half])
